import numpy as np
import ml_dtypes


def mxq(x, axis, fmt="e4m3"):
    dtype, down = {"e4m3": (ml_dtypes.float8_e4m3fn, 7), "e5m2": (ml_dtypes.float8_e5m2, 14)}[fmt]
    v = np.moveaxis(np.asarray(x, np.float32).astype(ml_dtypes.bfloat16).astype(np.float64), axis, -1)
    blocks = v.reshape(v.shape[:-1] + (-1, 32))
    amax = np.abs(blocks).max(-1, keepdims=True)
    byte = np.maximum(np.where(amax > 0, np.frexp(amax)[1] - 1 + 127, 0) - down, 1)
    scale = np.exp2(byte - 127.0)
    codes = (blocks / scale).astype(np.float32).astype(dtype).astype(np.float64)
    return np.moveaxis((codes * scale).reshape(v.shape), -1, axis)


WIDE = False


def mx_kscale(k):
    if not WIDE:
        return np.ones(k)
    levels = np.array([10, -10, 5, -5, 0])
    if k % 512:
        return np.exp2(np.random.permutation(np.resize(levels, k // 32))).repeat(32)
    a = np.empty((k // 512, 16))
    for p in range(k // 512):
        a[p, :8] = np.random.permutation(np.resize(levels, 8))
        for g in range(8):
            far = levels[np.abs(levels - a[p, g]) >= 10]
            a[p, g + 8] = far[np.random.randint(len(far))]
    return np.exp2(a.ravel()).repeat(32)


def f64(x):
    return np.asarray(x).astype(np.float64)


E2M1 = np.array([0.0, 0.5, 1.0, 1.5, 2.0, 3.0, 4.0, 6.0, -0.0, -0.5, -1.0, -1.5, -2.0, -3.0, -4.0, -6.0])


def pack_weight(w, fmt):
    k, n = w.shape
    w = f64(np.asarray(w, np.float32).astype(ml_dtypes.bfloat16)).reshape(k // 32, 32, n)
    amax = np.abs(w).max(1)
    if fmt == "e4m3":
        byte = np.frexp(amax)[1] - 1 + 127 - 7
    else:
        mant, ex = np.frexp(amax / 6.0)
        byte = np.where(mant > 0.5, ex, ex - 1) + 127
    byte = np.clip(np.where(amax > 0, byte, 1), 1, 254)
    scaled = (w * np.exp2(127.0 - byte)[:, None, :]).reshape(k, n).astype(np.float32)
    by_word = np.ascontiguousarray(scaled.reshape(k // 512, 128, 4, n).transpose(0, 1, 3, 2))
    if fmt == "e4m3":
        words = by_word.astype(ml_dtypes.float8_e4m3fn).view(np.uint8)
    else:
        c = by_word.astype(ml_dtypes.float4_e2m1fn).view(np.uint8) & 0xF
        words = (c[..., 0::2] | (c[..., 1::2] << 4)).reshape(k // 512, 128, 2 * n)
    return np.ascontiguousarray(words), np.ascontiguousarray(byte.astype(np.uint8).reshape(k // 512, 16, n))


def unpack_weight(words, scales, fmt):
    g, _, n = scales.shape
    words = np.ascontiguousarray(words).reshape(g, 128, n, -1)
    if fmt == "e4m3":
        vals = words.view(ml_dtypes.float8_e4m3fn).astype(np.float64)
    else:
        nib = np.empty((g, 128, n, 4), np.uint8)
        nib[..., 0::2] = words & 0xF
        nib[..., 1::2] = words >> 4
        vals = E2M1[nib]
    vals = vals * np.repeat(np.exp2(scales.astype(np.float64) - 127.0), 8, axis=1)[..., None]
    return vals.transpose(0, 1, 3, 2).reshape(g * 512, n)


K, M, T = 2048, 512, 1024


def setup_inputs():
    n = np.random.standard_normal
    s = mx_kscale(K)[:, None]
    w = n((K, M)) / np.sqrt(K) / s
    w4 = pack_weight(w, "e2m1")
    rest = w - unpack_weight(*w4, "e2m1")
    p_r8 = pack_weight(rest, "e4m3")
    return {
        "x": (n((K, T)) * s).astype(np.float32),
        "w4_words": w4[0],
        "w4_scales": w4[1],
        "r8_words": p_r8[0],
        "r8_scales": p_r8[1],
        "g": (n((512, 1024))).astype(np.float32),
    }


def reference(x, w4_words, w4_scales, r8_words, r8_scales, g):
    x_ = mxq(f64(x), 0, "e4m3")
    w4_ = unpack_weight(w4_words, w4_scales, "e2m1")
    r8_ = unpack_weight(r8_words, r8_scales, "e4m3")
    y = w4_.T @ x_ + r8_.T @ x_
    return f64(g) * y

@@ -1,0 +1,175 @@
+from contextlib import ExitStack
+
+import concourse.mybir as mybir
+
+K, N, T = 2048, 512, 1024
+
+F32 = mybir.dt.float32
+BF16 = mybir.dt.bfloat16
+I32 = mybir.dt.int32
+U32 = mybir.dt.uint32
+U8 = mybir.dt.uint8
+FP8X4 = mybir.dt.float8_e4m3fn_x4
+FP4X4 = mybir.dt.float4_e2m1fn_x4
+
+FLOPS = 2 * 2 * K * N * T
+
+P = 128
+PACK = 4
+K_PASS = P * PACK
+PASSES = K // K_PASS
+M_TILES = N // P
+T_TILE = 512
+HALVES = T // T_TILE
+QUADS = 4
+
+V_COLS = 336
+V_CUT = 168
+
+
+def tile_mix_resid_fm_mul_kernel(tc, x, w4_words, w4_scales, r8_words, r8_scales, g, out):
+    nc = tc.nc
+    with ExitStack() as ctx:
+        keep = ctx.enter_context(tc.tile_pool(name="keep", bufs=1))
+        psum = ctx.enter_context(tc.psum_pool(name="psum", bufs=1))
+
+        r8_plane = keep.tile([P, N], U8, name="r8_plane", align_bytes=64)
+        w4_plane = keep.tile([P, PASSES, N], U8, name="w4_plane", align_bytes=64)
+        x_raw = []
+        r8_codes = []
+        w4_codes = []
+        for a in range(PASSES):
+            x_raw.append(keep.tile([P, PACK, T], F32, name="x_raw%d" % a, align_bytes=64))
+            r8_codes.append(keep.tile([P, 4 * N], U8, name="r8_codes%d" % a, align_bytes=64))
+            w4_codes.append(keep.tile([P, 2 * N], U8, name="w4_codes%d" % a, align_bytes=64))
+        grouped = {}
+        codes = {}
+        scales = {}
+        for a in range(PASSES):
+            for h in range(HALVES):
+                grouped[a, h] = keep.tile([P, T_TILE, PACK], BF16, name="grouped%d%d" % (a, h), align_bytes=64)
+                codes[a, h] = keep.tile([P, T_TILE], U32, name="codes%d%d" % (a, h), align_bytes=64)
+                scales[a, h] = keep.tile([P, T_TILE], U8, name="scales%d%d" % (a, h), align_bytes=64)
+        g_sb = []
+        o_sb = []
+        acc = {}
+        for m in range(M_TILES):
+            g_sb.append(keep.tile([P, T], F32, name="g%d" % m))
+            o_sb.append(keep.tile([P, T], F32, name="o%d" % m))
+            for h in range(HALVES):
+                acc[m, h] = psum.tile([P, T_TILE], F32, name="acc%d%d" % (m, h))
+
+        def load_x_half(a, h):
+            cols = slice(h * T_TILE, (h + 1) * T_TILE)
+            nc.sync.dma_start(
+                out=x_raw[a][:, :, cols],
+                in_=x[a * K_PASS : (a + 1) * K_PASS, cols].rearrange("(p j) t -> p j t", j=PACK),
+            )
+
+        def load_x(a):
+            nc.sync.dma_start(
+                out=x_raw[a][:], in_=x[a * K_PASS : (a + 1) * K_PASS, :].rearrange("(p j) t -> p j t", j=PACK)
+            )
+
+        def load_w(a):
+            nc.sync.dma_start(
+                out=r8_codes[a][:].bitcast(I32), in_=r8_words[a].rearrange("p n i -> p (n i)").bitcast(I32)
+            )
+            nc.sync.dma_start(out=w4_codes[a][:].bitcast(I32), in_=w4_words[a].bitcast(I32))
+
+        def interleave(copy, a, h, lo, hi):
+            copy(
+                out=grouped[a, h][:, lo:hi, :].rearrange("p (c i) j -> p c j i", i=4),
+                in_=x_raw[a][:, :, h * T_TILE + lo : h * T_TILE + hi].rearrange("p j (c i) -> p c j i", i=4),
+            )
+
+        def quantize(a, h):
+            nc.vector.quantize_mx(
+                out=codes[a, h][:].bitcast(FP8X4),
+                scales=scales[a, h][:],
+                in_=grouped[a, h][:].rearrange("p c j -> p (c j)"),
+            )
+
+        def prepare(a):
+            for h in range(HALVES):
+                interleave(nc.scalar.copy, a, h, V_COLS, T_TILE)
+            if a == 0:
+                interleave(nc.vector.tensor_copy, a, 0, 0, V_COLS)
+                quantize(a, 0)
+                interleave(nc.vector.tensor_copy, a, 1, 0, V_COLS)
+                quantize(a, 1)
+                return
+            interleave(nc.vector.tensor_copy, a, 0, 0, V_COLS)
+            interleave(nc.vector.tensor_copy, a, 1, 0, V_CUT)
+            quantize(a, 0)
+            interleave(nc.vector.tensor_copy, a, 1, V_CUT, V_COLS)
+            quantize(a, 1)
+
+        def multiply_r8(a, m, h):
+            nc.tensor.matmul_mx(
+                out=acc[m, h][:],
+                lhsT=r8_codes[a][:, 4 * P * m : 4 * P * (m + 1)].bitcast(FP8X4),
+                lhsT_scale=r8_plane[4 * a : P, P * m : P * (m + 1)],
+                rhs=codes[a, h][:].bitcast(FP8X4),
+                rhs_scale=scales[a, h][:],
+                start=(a == 0),
+                stop=False,
+            )
+
+        def multiply_w4(a, m, h):
+            nc.tensor.matmul_mx(
+                out=acc[m, h][:],
+                lhsT=w4_codes[a][:, 2 * P * m : 2 * P * (m + 1)].bitcast(FP4X4),
+                lhsT_scale=w4_plane[:, a, P * m : P * (m + 1)],
+                rhs=codes[a, h][:].bitcast(FP8X4),
+                rhs_scale=scales[a, h][:],
+                start=False,
+                stop=(a == PASSES - 1),
+            )
+
+        with tc.manual_schedule():
+            nc.vector.memset(r8_plane[:].bitcast(I32), 0)
+            nc.vector.memset(w4_plane[:].rearrange("p a n -> p (a n)").bitcast(I32), 0)
+
+            load_x_half(0, 0)
+            for q in range(QUADS):
+                nc.scalar.dma_start(
+                    out=r8_plane[:].bitcast(I32)[32 * q : 32 * q + 16, :],
+                    in_=r8_scales[:, 4 * q : 4 * q + 4, :].bitcast(I32),
+                )
+            for q in range(QUADS):
+                queue = nc.scalar if q < QUADS - 1 else nc.gpsimd
+                queue.dma_start(
+                    out=w4_plane[32 * q : 32 * q + 4, :, :].bitcast(I32),
+                    in_=w4_scales[:, 4 * q : 4 * q + 4, :].rearrange("a r n -> r a n").bitcast(I32),
+                )
+            load_w(0)
+            load_x_half(0, 1)
+            for a in range(1, PASSES):
+                load_w(a)
+                load_x(a)
+            for m in range(M_TILES):
+                nc.sync.dma_start(out=g_sb[m][:], in_=g[m * P : (m + 1) * P, :])
+
+            for a in range(PASSES - 1):
+                prepare(a)
+                for h in range(HALVES):
+                    for m in range(M_TILES):
+                        multiply_r8(a, m, h)
+                    for m in range(M_TILES):
+                        multiply_w4(a, m, h)
+
+            last = PASSES - 1
+            prepare(last)
+            for m in range(M_TILES):
+                for h in range(HALVES):
+                    multiply_r8(last, m, h)
+                    multiply_w4(last, m, h)
+                    cols = slice(h * T_TILE, (h + 1) * T_TILE)
+                    nc.vector.tensor_tensor(
+                        out=o_sb[m][:, cols], in0=acc[m, h][:], in1=g_sb[m][:, cols], op=mybir.AluOpType.mult
+                    )
+                    if m == M_TILES - 1:
+                        nc.sync.dma_start(out=out[m * P : (m + 1) * P, cols], in_=o_sb[m][:, cols])
+                if m < M_TILES - 1:
+                    nc.sync.dma_start(out=out[m * P : (m + 1) * P, :], in_=o_sb[m][:])

@@ -23,6 +23,7 @@ T_TILE = 512
 HALVES = T // T_TILE
 QUADS = 4
 
+SPLIT = (0, 3)
 V_COLS = 336
 V_CUT = 168
 
@@ -35,11 +36,21 @@ def tile_mix_resid_fm_mul_kernel(tc, x, w4_words, w4_scales, r8_words, r8_scales
 
         r8_plane = keep.tile([P, N], U8, name="r8_plane", align_bytes=64)
         w4_plane = keep.tile([P, PASSES, N], U8, name="w4_plane", align_bytes=64)
-        x_raw = []
+        warm = keep.tile([P, 8], F32, name="warm")
+        x_raw = {}
+        x_whole = {}
         r8_codes = []
         w4_codes = []
         for a in range(PASSES):
-            x_raw.append(keep.tile([P, PACK, T], F32, name="x_raw%d" % a, align_bytes=64))
+            if a in SPLIT:
+                for h in range(HALVES):
+                    name = "x_raw%d%d" % (a, h)
+                    x_raw[a, h] = keep.tile([P, PACK, T_TILE], F32, name=name, align_bytes=64)
+            else:
+                whole = keep.tile([P, PACK, T], F32, name="x_raw%d" % a, align_bytes=64)
+                for h in range(HALVES):
+                    x_raw[a, h] = whole[:, :, h * T_TILE : (h + 1) * T_TILE]
+                x_whole[a] = whole
             r8_codes.append(keep.tile([P, 4 * N], U8, name="r8_codes%d" % a, align_bytes=64))
             w4_codes.append(keep.tile([P, 2 * N], U8, name="w4_codes%d" % a, align_bytes=64))
         grouped = {}
@@ -62,13 +73,13 @@ def tile_mix_resid_fm_mul_kernel(tc, x, w4_words, w4_scales, r8_words, r8_scales
         def load_x_half(a, h):
             cols = slice(h * T_TILE, (h + 1) * T_TILE)
             nc.sync.dma_start(
-                out=x_raw[a][:, :, cols],
+                out=x_raw[a, h][:],
                 in_=x[a * K_PASS : (a + 1) * K_PASS, cols].rearrange("(p j) t -> p j t", j=PACK),
             )
 
         def load_x(a):
             nc.sync.dma_start(
-                out=x_raw[a][:], in_=x[a * K_PASS : (a + 1) * K_PASS, :].rearrange("(p j) t -> p j t", j=PACK)
+                out=x_whole[a][:], in_=x[a * K_PASS : (a + 1) * K_PASS, :].rearrange("(p j) t -> p j t", j=PACK)
             )
 
         def load_w(a):
@@ -80,7 +91,7 @@ def tile_mix_resid_fm_mul_kernel(tc, x, w4_words, w4_scales, r8_words, r8_scales
         def interleave(copy, a, h, lo, hi):
             copy(
                 out=grouped[a, h][:, lo:hi, :].rearrange("p (c i) j -> p c j i", i=4),
-                in_=x_raw[a][:, :, h * T_TILE + lo : h * T_TILE + hi].rearrange("p j (c i) -> p c j i", i=4),
+                in_=x_raw[a, h][:, :, lo:hi].rearrange("p j (c i) -> p c j i", i=4),
             )
 
         def quantize(a, h):
@@ -93,12 +104,6 @@ def tile_mix_resid_fm_mul_kernel(tc, x, w4_words, w4_scales, r8_words, r8_scales
         def prepare(a):
             for h in range(HALVES):
                 interleave(nc.scalar.copy, a, h, V_COLS, T_TILE)
-            if a == 0:
-                interleave(nc.vector.tensor_copy, a, 0, 0, V_COLS)
-                quantize(a, 0)
-                interleave(nc.vector.tensor_copy, a, 1, 0, V_COLS)
-                quantize(a, 1)
-                return
             interleave(nc.vector.tensor_copy, a, 0, 0, V_COLS)
             interleave(nc.vector.tensor_copy, a, 1, 0, V_CUT)
             quantize(a, 0)
@@ -127,49 +132,64 @@ def tile_mix_resid_fm_mul_kernel(tc, x, w4_words, w4_scales, r8_words, r8_scales
                 stop=(a == PASSES - 1),
             )
 
+        def prepare_half(a, h):
+            interleave(nc.scalar.copy, a, h, V_COLS, T_TILE)
+            interleave(nc.vector.tensor_copy, a, h, 0, V_COLS)
+            quantize(a, h)
+
+        def multiply_half(a, h):
+            if a == PASSES - 1:
+                for m in range(M_TILES):
+                    multiply_r8(a, m, h)
+                    multiply_w4(a, m, h)
+            else:
+                for m in range(M_TILES):
+                    multiply_r8(a, m, h)
+                for m in range(M_TILES):
+                    multiply_w4(a, m, h)
+
         with tc.manual_schedule():
+            nc.vector.memset(warm[:], 0.0)
+            nc.scalar.copy(out=warm[:, 0:1], in_=warm[:, 4:5])
             nc.vector.memset(r8_plane[:].bitcast(I32), 0)
             nc.vector.memset(w4_plane[:].rearrange("p a n -> p (a n)").bitcast(I32), 0)
 
             load_x_half(0, 0)
             for q in range(QUADS):
-                nc.scalar.dma_start(
+                nc.sync.dma_start(
                     out=r8_plane[:].bitcast(I32)[32 * q : 32 * q + 16, :],
                     in_=r8_scales[:, 4 * q : 4 * q + 4, :].bitcast(I32),
                 )
+            load_w(0)
+            load_x_half(0, 1)
             for q in range(QUADS):
-                queue = nc.scalar if q < QUADS - 1 else nc.gpsimd
-                queue.dma_start(
+                nc.sync.dma_start(
                     out=w4_plane[32 * q : 32 * q + 4, :, :].bitcast(I32),
                     in_=w4_scales[:, 4 * q : 4 * q + 4, :].rearrange("a r n -> r a n").bitcast(I32),
                 )
-            load_w(0)
-            load_x_half(0, 1)
-            for a in range(1, PASSES):
-                load_w(a)
-                load_x(a)
+            load_x(1)
+            load_w(1)
+            load_x(2)
+            load_w(2)
+            load_w(3)
+            for h in range(HALVES):
+                load_x_half(3, h)
             for m in range(M_TILES):
                 nc.sync.dma_start(out=g_sb[m][:], in_=g[m * P : (m + 1) * P, :])
 
-            for a in range(PASSES - 1):
+            for h in range(HALVES):
+                prepare_half(0, h)
+                multiply_half(0, h)
+            for a in range(1, PASSES - 1):
                 prepare(a)
                 for h in range(HALVES):
-                    for m in range(M_TILES):
-                        multiply_r8(a, m, h)
-                    for m in range(M_TILES):
-                        multiply_w4(a, m, h)
-
-            last = PASSES - 1
-            prepare(last)
-            for m in range(M_TILES):
-                for h in range(HALVES):
-                    multiply_r8(last, m, h)
-                    multiply_w4(last, m, h)
-                    cols = slice(h * T_TILE, (h + 1) * T_TILE)
-                    nc.vector.tensor_tensor(
-                        out=o_sb[m][:, cols], in0=acc[m, h][:], in1=g_sb[m][:, cols], op=mybir.AluOpType.mult
-                    )
-                    if m == M_TILES - 1:
-                        nc.sync.dma_start(out=out[m * P : (m + 1) * P, cols], in_=o_sb[m][:, cols])
-                if m < M_TILES - 1:
-                    nc.sync.dma_start(out=out[m * P : (m + 1) * P, :], in_=o_sb[m][:])
+                    multiply_half(a, h)
+            for h in range(HALVES):
+                prepare_half(PASSES - 1, h)
+                multiply_half(PASSES - 1, h)
+            for m, h in ((0, 0), (1, 0), (0, 1), (1, 1), (2, 0), (2, 1), (3, 0), (3, 1)):
+                cols = slice(h * T_TILE, (h + 1) * T_TILE)
+                nc.vector.tensor_tensor(
+                    out=o_sb[m][:, cols], in0=acc[m, h][:], in1=g_sb[m][:, cols], op=mybir.AluOpType.mult
+                )
+                nc.sync.dma_start(out=out[m * P : (m + 1) * P, cols], in_=o_sb[m][:, cols])

@@ -23,9 +23,9 @@ T_TILE = 512
 HALVES = T // T_TILE
 QUADS = 4
 
-SPLIT = (0, 3)
-V_COLS = 336
-V_CUT = 168
+ORDER = ((0, 0), (1, 0), (0, 1), (1, 1), (2, 0), (2, 1), (3, 0), (3, 1))
+CHUNK = 256
+V_COLS = 168
 
 
 def tile_mix_resid_fm_mul_kernel(tc, x, w4_words, w4_scales, r8_words, r8_scales, g, out):
@@ -37,20 +37,11 @@ def tile_mix_resid_fm_mul_kernel(tc, x, w4_words, w4_scales, r8_words, r8_scales
         r8_plane = keep.tile([P, N], U8, name="r8_plane", align_bytes=64)
         w4_plane = keep.tile([P, PASSES, N], U8, name="w4_plane", align_bytes=64)
         warm = keep.tile([P, 8], F32, name="warm")
-        x_raw = {}
-        x_whole = {}
+        x_raw = []
         r8_codes = []
         w4_codes = []
         for a in range(PASSES):
-            if a in SPLIT:
-                for h in range(HALVES):
-                    name = "x_raw%d%d" % (a, h)
-                    x_raw[a, h] = keep.tile([P, PACK, T_TILE], F32, name=name, align_bytes=64)
-            else:
-                whole = keep.tile([P, PACK, T], F32, name="x_raw%d" % a, align_bytes=64)
-                for h in range(HALVES):
-                    x_raw[a, h] = whole[:, :, h * T_TILE : (h + 1) * T_TILE]
-                x_whole[a] = whole
+            x_raw.append(keep.tile([P, PACK, T], F32, name="x_raw%d" % a, align_bytes=64))
             r8_codes.append(keep.tile([P, 4 * N], U8, name="r8_codes%d" % a, align_bytes=64))
             w4_codes.append(keep.tile([P, 2 * N], U8, name="w4_codes%d" % a, align_bytes=64))
         grouped = {}
@@ -70,16 +61,9 @@ def tile_mix_resid_fm_mul_kernel(tc, x, w4_words, w4_scales, r8_words, r8_scales
             for h in range(HALVES):
                 acc[m, h] = psum.tile([P, T_TILE], F32, name="acc%d%d" % (m, h))
 
-        def load_x_half(a, h):
-            cols = slice(h * T_TILE, (h + 1) * T_TILE)
-            nc.sync.dma_start(
-                out=x_raw[a, h][:],
-                in_=x[a * K_PASS : (a + 1) * K_PASS, cols].rearrange("(p j) t -> p j t", j=PACK),
-            )
-
         def load_x(a):
             nc.sync.dma_start(
-                out=x_whole[a][:], in_=x[a * K_PASS : (a + 1) * K_PASS, :].rearrange("(p j) t -> p j t", j=PACK)
+                out=x_raw[a][:], in_=x[a * K_PASS : (a + 1) * K_PASS, :].rearrange("(p j) t -> p j t", j=PACK)
             )
 
         def load_w(a):
@@ -91,24 +75,24 @@ def tile_mix_resid_fm_mul_kernel(tc, x, w4_words, w4_scales, r8_words, r8_scales
         def interleave(copy, a, h, lo, hi):
             copy(
                 out=grouped[a, h][:, lo:hi, :].rearrange("p (c i) j -> p c j i", i=4),
-                in_=x_raw[a, h][:, :, lo:hi].rearrange("p j (c i) -> p c j i", i=4),
+                in_=x_raw[a][:, :, h * T_TILE + lo : h * T_TILE + hi].rearrange("p j (c i) -> p c j i", i=4),
             )
 
-        def quantize(a, h):
+        def quantize(a, h, lo, hi):
             nc.vector.quantize_mx(
-                out=codes[a, h][:].bitcast(FP8X4),
-                scales=scales[a, h][:],
-                in_=grouped[a, h][:].rearrange("p c j -> p (c j)"),
+                out=codes[a, h][:, lo:hi].bitcast(FP8X4),
+                scales=scales[a, h][:, lo:hi],
+                in_=grouped[a, h][:, lo:hi, :].rearrange("p c j -> p (c j)"),
             )
 
         def prepare(a):
             for h in range(HALVES):
-                interleave(nc.scalar.copy, a, h, V_COLS, T_TILE)
-            interleave(nc.vector.tensor_copy, a, 0, 0, V_COLS)
-            interleave(nc.vector.tensor_copy, a, 1, 0, V_CUT)
-            quantize(a, 0)
-            interleave(nc.vector.tensor_copy, a, 1, V_CUT, V_COLS)
-            quantize(a, 1)
+                for lo in range(0, T_TILE, CHUNK):
+                    interleave(nc.scalar.copy, a, h, lo + V_COLS, lo + CHUNK)
+                for lo in range(0, T_TILE, CHUNK):
+                    interleave(nc.vector.tensor_copy, a, h, lo, lo + V_COLS)
+                for lo in range(0, T_TILE, CHUNK):
+                    quantize(a, h, lo, lo + CHUNK)
 
         def multiply_r8(a, m, h):
             nc.tensor.matmul_mx(
@@ -132,62 +116,46 @@ def tile_mix_resid_fm_mul_kernel(tc, x, w4_words, w4_scales, r8_words, r8_scales
                 stop=(a == PASSES - 1),
             )
 
-        def prepare_half(a, h):
-            interleave(nc.scalar.copy, a, h, V_COLS, T_TILE)
-            interleave(nc.vector.tensor_copy, a, h, 0, V_COLS)
-            quantize(a, h)
-
-        def multiply_half(a, h):
-            if a == PASSES - 1:
-                for m in range(M_TILES):
-                    multiply_r8(a, m, h)
-                    multiply_w4(a, m, h)
-            else:
-                for m in range(M_TILES):
-                    multiply_r8(a, m, h)
-                for m in range(M_TILES):
-                    multiply_w4(a, m, h)
-
         with tc.manual_schedule():
             nc.vector.memset(warm[:], 0.0)
             nc.scalar.copy(out=warm[:, 0:1], in_=warm[:, 4:5])
             nc.vector.memset(r8_plane[:].bitcast(I32), 0)
             nc.vector.memset(w4_plane[:].rearrange("p a n -> p (a n)").bitcast(I32), 0)
 
-            load_x_half(0, 0)
+            load_x(0)
             for q in range(QUADS):
                 nc.sync.dma_start(
                     out=r8_plane[:].bitcast(I32)[32 * q : 32 * q + 16, :],
                     in_=r8_scales[:, 4 * q : 4 * q + 4, :].bitcast(I32),
                 )
             load_w(0)
-            load_x_half(0, 1)
+            load_x(1)
             for q in range(QUADS):
                 nc.sync.dma_start(
                     out=w4_plane[32 * q : 32 * q + 4, :, :].bitcast(I32),
                     in_=w4_scales[:, 4 * q : 4 * q + 4, :].rearrange("a r n -> r a n").bitcast(I32),
                 )
-            load_x(1)
             load_w(1)
-            load_x(2)
-            load_w(2)
-            load_w(3)
-            for h in range(HALVES):
-                load_x_half(3, h)
+            for a in range(2, PASSES):
+                load_x(a)
+                load_w(a)
             for m in range(M_TILES):
                 nc.sync.dma_start(out=g_sb[m][:], in_=g[m * P : (m + 1) * P, :])
 
-            for h in range(HALVES):
-                prepare_half(0, h)
-                multiply_half(0, h)
-            for a in range(1, PASSES - 1):
+            for a in range(PASSES - 1):
                 prepare(a)
                 for h in range(HALVES):
-                    multiply_half(a, h)
-            for h in range(HALVES):
-                prepare_half(PASSES - 1, h)
-                multiply_half(PASSES - 1, h)
-            for m, h in ((0, 0), (1, 0), (0, 1), (1, 1), (2, 0), (2, 1), (3, 0), (3, 1)):
+                    for m in range(M_TILES):
+                        multiply_r8(a, m, h)
+                for h in range(HALVES):
+                    for m in range(M_TILES):
+                        multiply_w4(a, m, h)
+
+            prepare(PASSES - 1)
+            for m, h in ORDER:
+                multiply_r8(PASSES - 1, m, h)
+                multiply_w4(PASSES - 1, m, h)
+            for m, h in ORDER:
                 cols = slice(h * T_TILE, (h + 1) * T_TILE)
                 nc.vector.tensor_tensor(
                     out=o_sb[m][:, cols], in0=acc[m, h][:], in1=g_sb[m][:, cols], op=mybir.AluOpType.mult

@@ -26,6 +26,7 @@ QUADS = 4
 ORDER = ((0, 0), (1, 0), (0, 1), (1, 1), (2, 0), (2, 1), (3, 0), (3, 1))
 CHUNK = 256
 V_COLS = 168
+V_COLS_LAST = 112
 
 
 def tile_mix_resid_fm_mul_kernel(tc, x, w4_words, w4_scales, r8_words, r8_scales, g, out):
@@ -67,10 +68,10 @@ def tile_mix_resid_fm_mul_kernel(tc, x, w4_words, w4_scales, r8_words, r8_scales
             )
 
         def load_w(a):
+            nc.sync.dma_start(out=w4_codes[a][:].bitcast(I32), in_=w4_words[a].bitcast(I32))
             nc.sync.dma_start(
                 out=r8_codes[a][:].bitcast(I32), in_=r8_words[a].rearrange("p n i -> p (n i)").bitcast(I32)
             )
-            nc.sync.dma_start(out=w4_codes[a][:].bitcast(I32), in_=w4_words[a].bitcast(I32))
 
         def interleave(copy, a, h, lo, hi):
             copy(
@@ -87,10 +88,11 @@ def tile_mix_resid_fm_mul_kernel(tc, x, w4_words, w4_scales, r8_words, r8_scales
 
         def prepare(a):
             for h in range(HALVES):
+                v_cols = V_COLS_LAST if (a, h) == (PASSES - 1, 1) else V_COLS
                 for lo in range(0, T_TILE, CHUNK):
-                    interleave(nc.scalar.copy, a, h, lo + V_COLS, lo + CHUNK)
+                    interleave(nc.scalar.copy, a, h, lo + v_cols, lo + CHUNK)
                 for lo in range(0, T_TILE, CHUNK):
-                    interleave(nc.vector.tensor_copy, a, h, lo, lo + V_COLS)
+                    interleave(nc.vector.tensor_copy, a, h, lo, lo + v_cols)
                 for lo in range(0, T_TILE, CHUNK):
                     quantize(a, h, lo, lo + CHUNK)
 
@@ -101,8 +103,8 @@ def tile_mix_resid_fm_mul_kernel(tc, x, w4_words, w4_scales, r8_words, r8_scales
                 lhsT_scale=r8_plane[4 * a : P, P * m : P * (m + 1)],
                 rhs=codes[a, h][:].bitcast(FP8X4),
                 rhs_scale=scales[a, h][:],
-                start=(a == 0),
-                stop=False,
+                start=False,
+                stop=(a == PASSES - 1),
             )
 
         def multiply_w4(a, m, h):
@@ -112,8 +114,8 @@ def tile_mix_resid_fm_mul_kernel(tc, x, w4_words, w4_scales, r8_words, r8_scales
                 lhsT_scale=w4_plane[:, a, P * m : P * (m + 1)],
                 rhs=codes[a, h][:].bitcast(FP8X4),
                 rhs_scale=scales[a, h][:],
-                start=False,
-                stop=(a == PASSES - 1),
+                start=(a == 0),
+                stop=False,
             )
 
         with tc.manual_schedule():
@@ -124,17 +126,17 @@ def tile_mix_resid_fm_mul_kernel(tc, x, w4_words, w4_scales, r8_words, r8_scales
 
             load_x(0)
             for q in range(QUADS):
-                nc.sync.dma_start(
+                nc.gpsimd.dma_start(
                     out=r8_plane[:].bitcast(I32)[32 * q : 32 * q + 16, :],
                     in_=r8_scales[:, 4 * q : 4 * q + 4, :].bitcast(I32),
                 )
-            load_w(0)
-            load_x(1)
             for q in range(QUADS):
                 nc.sync.dma_start(
                     out=w4_plane[32 * q : 32 * q + 4, :, :].bitcast(I32),
                     in_=w4_scales[:, 4 * q : 4 * q + 4, :].rearrange("a r n -> r a n").bitcast(I32),
                 )
+            load_w(0)
+            load_x(1)
             load_w(1)
             for a in range(2, PASSES):
                 load_x(a)
@@ -146,15 +148,15 @@ def tile_mix_resid_fm_mul_kernel(tc, x, w4_words, w4_scales, r8_words, r8_scales
                 prepare(a)
                 for h in range(HALVES):
                     for m in range(M_TILES):
-                        multiply_r8(a, m, h)
+                        multiply_w4(a, m, h)
                 for h in range(HALVES):
                     for m in range(M_TILES):
-                        multiply_w4(a, m, h)
+                        multiply_r8(a, m, h)
 
             prepare(PASSES - 1)
             for m, h in ORDER:
-                multiply_r8(PASSES - 1, m, h)
                 multiply_w4(PASSES - 1, m, h)
+                multiply_r8(PASSES - 1, m, h)
             for m, h in ORDER:
                 cols = slice(h * T_TILE, (h + 1) * T_TILE)
                 nc.vector.tensor_tensor(

@@ -26,7 +26,7 @@ QUADS = 4
 ORDER = ((0, 0), (1, 0), (0, 1), (1, 1), (2, 0), (2, 1), (3, 0), (3, 1))
 CHUNK = 256
 V_COLS = 168
-V_COLS_LAST = 112
+V_COLS_LAST = 144
 
 
 def tile_mix_resid_fm_mul_kernel(tc, x, w4_words, w4_scales, r8_words, r8_scales, g, out):
@@ -68,10 +68,10 @@ def tile_mix_resid_fm_mul_kernel(tc, x, w4_words, w4_scales, r8_words, r8_scales
             )
 
         def load_w(a):
-            nc.sync.dma_start(out=w4_codes[a][:].bitcast(I32), in_=w4_words[a].bitcast(I32))
             nc.sync.dma_start(
                 out=r8_codes[a][:].bitcast(I32), in_=r8_words[a].rearrange("p n i -> p (n i)").bitcast(I32)
             )
+            nc.sync.dma_start(out=w4_codes[a][:].bitcast(I32), in_=w4_words[a].bitcast(I32))
 
         def interleave(copy, a, h, lo, hi):
             copy(
@@ -103,8 +103,8 @@ def tile_mix_resid_fm_mul_kernel(tc, x, w4_words, w4_scales, r8_words, r8_scales
                 lhsT_scale=r8_plane[4 * a : P, P * m : P * (m + 1)],
                 rhs=codes[a, h][:].bitcast(FP8X4),
                 rhs_scale=scales[a, h][:],
-                start=False,
-                stop=(a == PASSES - 1),
+                start=(a == 0),
+                stop=False,
             )
 
         def multiply_w4(a, m, h):
@@ -114,8 +114,8 @@ def tile_mix_resid_fm_mul_kernel(tc, x, w4_words, w4_scales, r8_words, r8_scales
                 lhsT_scale=w4_plane[:, a, P * m : P * (m + 1)],
                 rhs=codes[a, h][:].bitcast(FP8X4),
                 rhs_scale=scales[a, h][:],
-                start=(a == 0),
-                stop=False,
+                start=False,
+                stop=(a == PASSES - 1),
             )
 
         with tc.manual_schedule():
@@ -126,17 +126,17 @@ def tile_mix_resid_fm_mul_kernel(tc, x, w4_words, w4_scales, r8_words, r8_scales
 
             load_x(0)
             for q in range(QUADS):
-                nc.gpsimd.dma_start(
+                nc.sync.dma_start(
                     out=r8_plane[:].bitcast(I32)[32 * q : 32 * q + 16, :],
                     in_=r8_scales[:, 4 * q : 4 * q + 4, :].bitcast(I32),
                 )
+            load_w(0)
+            load_x(1)
             for q in range(QUADS):
                 nc.sync.dma_start(
                     out=w4_plane[32 * q : 32 * q + 4, :, :].bitcast(I32),
                     in_=w4_scales[:, 4 * q : 4 * q + 4, :].rearrange("a r n -> r a n").bitcast(I32),
                 )
-            load_w(0)
-            load_x(1)
             load_w(1)
             for a in range(2, PASSES):
                 load_x(a)
@@ -148,18 +148,19 @@ def tile_mix_resid_fm_mul_kernel(tc, x, w4_words, w4_scales, r8_words, r8_scales
                 prepare(a)
                 for h in range(HALVES):
                     for m in range(M_TILES):
-                        multiply_w4(a, m, h)
+                        multiply_r8(a, m, h)
                 for h in range(HALVES):
                     for m in range(M_TILES):
-                        multiply_r8(a, m, h)
+                        multiply_w4(a, m, h)
 
             prepare(PASSES - 1)
             for m, h in ORDER:
-                multiply_w4(PASSES - 1, m, h)
                 multiply_r8(PASSES - 1, m, h)
+                multiply_w4(PASSES - 1, m, h)
             for m, h in ORDER:
                 cols = slice(h * T_TILE, (h + 1) * T_TILE)
                 nc.vector.tensor_tensor(
                     out=o_sb[m][:, cols], in0=acc[m, h][:], in1=g_sb[m][:, cols], op=mybir.AluOpType.mult
                 )
-                nc.sync.dma_start(out=out[m * P : (m + 1) * P, cols], in_=o_sb[m][:, cols])
+                queue = nc.sync if h == 0 else nc.scalar
+                queue.dma_start(out=out[m * P : (m + 1) * P, cols], in_=o_sb[m][:, cols])

from contextlib import ExitStack

import concourse.mybir as mybir

K, N, T = 2048, 512, 1024

F32 = mybir.dt.float32
BF16 = mybir.dt.bfloat16
I32 = mybir.dt.int32
U32 = mybir.dt.uint32
U8 = mybir.dt.uint8
FP8X4 = mybir.dt.float8_e4m3fn_x4
FP4X4 = mybir.dt.float4_e2m1fn_x4

FLOPS = 2 * 2 * K * N * T

P = 128
PACK = 4
K_PASS = P * PACK
PASSES = K // K_PASS
M_TILES = N // P
T_TILE = 512
HALVES = T // T_TILE
QUADS = 4

ORDER = ((0, 0), (1, 0), (0, 1), (1, 1), (2, 0), (2, 1), (3, 0), (3, 1))
CHUNK = 256
V_COLS = 168
V_COLS_LAST = 144


def tile_mix_resid_fm_mul_kernel(tc, x, w4_words, w4_scales, r8_words, r8_scales, g, out):
    nc = tc.nc
    with ExitStack() as ctx:
        keep = ctx.enter_context(tc.tile_pool(name="keep", bufs=1))
        psum = ctx.enter_context(tc.psum_pool(name="psum", bufs=1))

        r8_plane = keep.tile([P, N], U8, name="r8_plane", align_bytes=64)
        w4_plane = keep.tile([P, PASSES, N], U8, name="w4_plane", align_bytes=64)
        warm = keep.tile([P, 8], F32, name="warm")
        x_raw = []
        r8_codes = []
        w4_codes = []
        for a in range(PASSES):
            x_raw.append(keep.tile([P, PACK, T], F32, name="x_raw%d" % a, align_bytes=64))
            r8_codes.append(keep.tile([P, 4 * N], U8, name="r8_codes%d" % a, align_bytes=64))
            w4_codes.append(keep.tile([P, 2 * N], U8, name="w4_codes%d" % a, align_bytes=64))
        grouped = {}
        codes = {}
        scales = {}
        for a in range(PASSES):
            for h in range(HALVES):
                grouped[a, h] = keep.tile([P, T_TILE, PACK], BF16, name="grouped%d%d" % (a, h), align_bytes=64)
                codes[a, h] = keep.tile([P, T_TILE], U32, name="codes%d%d" % (a, h), align_bytes=64)
                scales[a, h] = keep.tile([P, T_TILE], U8, name="scales%d%d" % (a, h), align_bytes=64)
        g_sb = []
        o_sb = []
        acc = {}
        for m in range(M_TILES):
            g_sb.append(keep.tile([P, T], F32, name="g%d" % m))
            o_sb.append(keep.tile([P, T], F32, name="o%d" % m))
            for h in range(HALVES):
                acc[m, h] = psum.tile([P, T_TILE], F32, name="acc%d%d" % (m, h))

        def load_x(a):
            nc.sync.dma_start(
                out=x_raw[a][:], in_=x[a * K_PASS : (a + 1) * K_PASS, :].rearrange("(p j) t -> p j t", j=PACK)
            )

        def load_w(a):
            nc.sync.dma_start(
                out=r8_codes[a][:].bitcast(I32), in_=r8_words[a].rearrange("p n i -> p (n i)").bitcast(I32)
            )
            nc.sync.dma_start(out=w4_codes[a][:].bitcast(I32), in_=w4_words[a].bitcast(I32))

        def interleave(copy, a, h, lo, hi):
            copy(
                out=grouped[a, h][:, lo:hi, :].rearrange("p (c i) j -> p c j i", i=4),
                in_=x_raw[a][:, :, h * T_TILE + lo : h * T_TILE + hi].rearrange("p j (c i) -> p c j i", i=4),
            )

        def quantize(a, h, lo, hi):
            nc.vector.quantize_mx(
                out=codes[a, h][:, lo:hi].bitcast(FP8X4),
                scales=scales[a, h][:, lo:hi],
                in_=grouped[a, h][:, lo:hi, :].rearrange("p c j -> p (c j)"),
            )

        def prepare(a):
            for h in range(HALVES):
                v_cols = V_COLS_LAST if (a, h) == (PASSES - 1, 1) else V_COLS
                for lo in range(0, T_TILE, CHUNK):
                    interleave(nc.scalar.copy, a, h, lo + v_cols, lo + CHUNK)
                for lo in range(0, T_TILE, CHUNK):
                    interleave(nc.vector.tensor_copy, a, h, lo, lo + v_cols)
                for lo in range(0, T_TILE, CHUNK):
                    quantize(a, h, lo, lo + CHUNK)

        def multiply_r8(a, m, h):
            nc.tensor.matmul_mx(
                out=acc[m, h][:],
                lhsT=r8_codes[a][:, 4 * P * m : 4 * P * (m + 1)].bitcast(FP8X4),
                lhsT_scale=r8_plane[4 * a : P, P * m : P * (m + 1)],
                rhs=codes[a, h][:].bitcast(FP8X4),
                rhs_scale=scales[a, h][:],
                start=(a == 0),
                stop=False,
            )

        def multiply_w4(a, m, h):
            nc.tensor.matmul_mx(
                out=acc[m, h][:],
                lhsT=w4_codes[a][:, 2 * P * m : 2 * P * (m + 1)].bitcast(FP4X4),
                lhsT_scale=w4_plane[:, a, P * m : P * (m + 1)],
                rhs=codes[a, h][:].bitcast(FP8X4),
                rhs_scale=scales[a, h][:],
                start=False,
                stop=(a == PASSES - 1),
            )

        with tc.manual_schedule():
            nc.vector.memset(warm[:], 0.0)
            nc.scalar.copy(out=warm[:, 0:1], in_=warm[:, 4:5])
            nc.vector.memset(r8_plane[:].bitcast(I32), 0)
            nc.vector.memset(w4_plane[:].rearrange("p a n -> p (a n)").bitcast(I32), 0)

            load_x(0)
            for q in range(QUADS):
                nc.sync.dma_start(
                    out=r8_plane[:].bitcast(I32)[32 * q : 32 * q + 16, :],
                    in_=r8_scales[:, 4 * q : 4 * q + 4, :].bitcast(I32),
                )
            load_w(0)
            load_x(1)
            for q in range(QUADS):
                nc.sync.dma_start(
                    out=w4_plane[32 * q : 32 * q + 4, :, :].bitcast(I32),
                    in_=w4_scales[:, 4 * q : 4 * q + 4, :].rearrange("a r n -> r a n").bitcast(I32),
                )
            load_w(1)
            for a in range(2, PASSES):
                load_x(a)
                load_w(a)
            for m in range(M_TILES):
                nc.sync.dma_start(out=g_sb[m][:], in_=g[m * P : (m + 1) * P, :])

            for a in range(PASSES - 1):
                prepare(a)
                for h in range(HALVES):
                    for m in range(M_TILES):
                        multiply_r8(a, m, h)
                for h in range(HALVES):
                    for m in range(M_TILES):
                        multiply_w4(a, m, h)

            prepare(PASSES - 1)
            for m, h in ORDER:
                multiply_r8(PASSES - 1, m, h)
                multiply_w4(PASSES - 1, m, h)
            for m, h in ORDER:
                cols = slice(h * T_TILE, (h + 1) * T_TILE)
                nc.vector.tensor_tensor(
                    out=o_sb[m][:, cols], in0=acc[m, h][:], in1=g_sb[m][:, cols], op=mybir.AluOpType.mult
                )
                queue = nc.sync if h == 0 else nc.scalar
                queue.dma_start(out=out[m * P : (m + 1) * P, cols], in_=o_sb[m][:, cols])
